import numpy as np
import ml_dtypes


def mxq(x, axis, fmt="e4m3"):
    dtype, down = {"e4m3": (ml_dtypes.float8_e4m3fn, 7), "e5m2": (ml_dtypes.float8_e5m2, 14)}[fmt]
    v = np.moveaxis(np.asarray(x, np.float32).astype(ml_dtypes.bfloat16).astype(np.float64), axis, -1)
    blocks = v.reshape(v.shape[:-1] + (-1, 32))
    amax = np.abs(blocks).max(-1, keepdims=True)
    byte = np.maximum(np.where(amax > 0, np.frexp(amax)[1] - 1 + 127, 0) - down, 1)
    scale = np.exp2(byte - 127.0)
    codes = (blocks / scale).astype(np.float32).astype(dtype).astype(np.float64)
    return np.moveaxis((codes * scale).reshape(v.shape), -1, axis)


WIDE = False


def mx_kscale(k):
    if not WIDE:
        return np.ones(k)
    levels = np.array([10, -10, 5, -5, 0])
    if k % 512:
        return np.exp2(np.random.permutation(np.resize(levels, k // 32))).repeat(32)
    a = np.empty((k // 512, 16))
    for p in range(k // 512):
        a[p, :8] = np.random.permutation(np.resize(levels, 8))
        for g in range(8):
            far = levels[np.abs(levels - a[p, g]) >= 10]
            a[p, g + 8] = far[np.random.randint(len(far))]
    return np.exp2(a.ravel()).repeat(32)


def f64(x):
    return np.asarray(x).astype(np.float64)


def striped(idx):
    return np.tile(idx.reshape(-1, 16).T, (8, 1)).astype(np.uint16)


def unstriped(offs):
    return offs[:16].T.reshape(-1).astype(np.int64)


def gelu(v):
    return 0.5 * v * (1.0 + np.tanh(np.sqrt(2.0 / np.pi) * (v + 0.044715 * v**3)))


K, T, S, V, H, N = 1024, 2048, 1024, 256, 512, 256


def setup_inputs():
    n = np.random.standard_normal
    s = mx_kscale(K)[:, None]
    u = mx_kscale(H)
    return {
        "xT": (n((K, T)) * s).astype(np.float32),
        "w1": (n((K, H)) / np.sqrt(K) / s * u).astype(np.float32),
        "w2": (n((H, N)) / np.sqrt(2 * H) / u[:, None]).astype(np.float32),
        "w3": (n((H, N)) / np.sqrt(2 * H) / u[:, None]).astype(np.float32),
        "offs": striped(np.random.permutation(T)[:S]),
    }


def reference(xT, w1, w2, w3, offs):
    xq = mxq(f64(xT)[:, unstriped(offs)], 0, "e4m3")
    h = gelu(mxq(f64(w1), 0, "e4m3").T @ xq)
    mean = (h[:, :V] + h[:, V:2 * V] + h[:, 2 * V:3 * V] + h[:, 3 * V:4 * V]) / 4
    dev = np.sqrt(((h[:, :V] - mean) ** 2 + (h[:, V:2 * V] - mean) ** 2 + (h[:, 2 * V:3 * V] - mean) ** 2 + (h[:, 3 * V:4 * V] - mean) ** 2) / 4)
    return mxq(f64(w2), 0, "e4m3").T @ mxq(mean, 0, "e4m3") + mxq(f64(w3), 0, "e4m3").T @ mxq(dev, 0, "e4m3")

@@ -1,0 +1,237 @@
+from contextlib import ExitStack
+
+import concourse.mybir as mybir
+
+K, T, S, V, H, N = 1024, 2048, 1024, 256, 512, 256
+D = S // V
+FLOPS = 2 * K * H * S + 2 * 2 * H * N * V
+
+F32 = mybir.dt.float32
+BF16 = mybir.dt.bfloat16
+I32 = mybir.dt.int32
+U32 = mybir.dt.uint32
+U16 = mybir.dt.uint16
+U8 = mybir.dt.uint8
+FP8X4 = mybir.dt.float8_e4m3fn_x4
+ACT = mybir.ActivationFunctionType
+ALU = mybir.AluOpType
+
+P = 128
+PACK = 4
+K_PASS = P * PACK
+PASSES = K // K_PASS
+VH = 128
+HALVES = V // VH
+CHUNKS = ((512, 512, 512, 512), (512, 512, 512, 256, 256))
+VECTOR_COLUMNS = ((0, 512, 0, 512), (0, 0, 256, 128, 160))
+
+
+def weave(nc, on_vector, out, in_):
+    if on_vector:
+        nc.vector.tensor_copy(out=out, in_=in_)
+    else:
+        nc.scalar.copy(out=out, in_=in_)
+
+
+def tile_picked_statpool_gelu_e_kernel(tc, xT, w1, w2, w3, offs, out):
+    nc = tc.nc
+    with ExitStack() as ctx:
+        keep = ctx.enter_context(tc.tile_pool(name="keep", bufs=1))
+        ring = ctx.enter_context(tc.tile_pool(name="ring", bufs=3))
+        relay = ctx.enter_context(tc.tile_pool(name="relay", bufs=1))
+        psum = ctx.enter_context(tc.psum_pool(name="psum", bufs=1))
+
+        offsets = keep.tile([P, S // 16], U16, name="offsets")
+
+        def load(rows, name):
+            raw = keep.tile([P, PACK, rows.shape[1]], F32, name=name)
+            nc.sync.dma_start(out=raw[:], in_=rows.rearrange("(p j) w -> p j w", j=PACK))
+            return raw
+
+        def load_x(z):
+            tiles, c0 = [], 0
+            for n, width in enumerate(CHUNKS[z]):
+                tiles.append(load(xT[z * K_PASS : (z + 1) * K_PASS, c0 : c0 + width], "x_raw_%d_%d" % (z, n)))
+                c0 += width
+            return tiles
+
+        x_raw = [load_x(0)]
+        nc.sync.dma_start(offsets[:], offs)
+        w1_raw = [[load(w1[0:K_PASS, :], "w1_raw_0")]]
+        x_raw.append(load_x(1))
+        w1_raw.append([load(w1[K_PASS:K, u * 256 : (u + 1) * 256], "w1_raw_1_%d" % u) for u in range(2)])
+        w23_raw = [load(w2, "w2_raw"), load(w3, "w3_raw")]
+
+        warm = keep.tile([P, 2], F32, name="warm")
+        nc.gpsimd.memset(warm[:, 0:1], 0.0)
+        nc.scalar.activation(out=warm[:, 1:2], in_=warm[:, 0:1], func=ACT.Gelu_apprx_tanh)
+
+        x_words = [keep.tile([P, T], U32, name="x_words_%d" % z, align_bytes=64) for z in range(PASSES)]
+        x_bytes = [keep.tile([P, T], U8, name="x_bytes_%d" % z, align_bytes=64) for z in range(PASSES)]
+        for z in range(PASSES):
+            nc.gpsimd.memset(x_bytes[z][:].bitcast(I32), 0)
+
+        def quantize_x(z):
+            c0 = 0
+            for n, width in enumerate(CHUNKS[z]):
+                woven = ring.tile([P, width * PACK], BF16, name="x_woven", align_bytes=64)
+                cut = VECTOR_COLUMNS[z][n]
+                for on_vector, lo, hi in ((True, 0, cut), (False, cut, width)):
+                    if hi > lo:
+                        weave(
+                            nc,
+                            on_vector,
+                            woven[:, lo * PACK : hi * PACK].rearrange("p (c i j) -> p c j i", i=4, j=PACK),
+                            x_raw[z][n][:, :, lo:hi].rearrange("p j (c i) -> p c j i", i=4),
+                        )
+                nc.vector.quantize_mx(
+                    out=x_words[z][:, c0 : c0 + width].bitcast(FP8X4),
+                    scales=x_bytes[z][:, c0 : c0 + width],
+                    in_=woven[:],
+                )
+                c0 += width
+
+        def quantize_w1(z):
+            if z == 0:
+                woven = keep.tile([P, H * PACK], BF16, name="w1_woven_0", align_bytes=64)
+            else:
+                woven = relay.tile([P, H * PACK], BF16, name="w1_woven_1", align_bytes=64, offset=0)
+            view = woven[:].rearrange("p (t m j) -> p m j t", t=PACK, j=PACK)
+            parts = len(w1_raw[z])
+            for u in range(parts):
+                m = P // parts
+                nc.scalar.copy(
+                    out=view[:, u * m : (u + 1) * m],
+                    in_=w1_raw[z][u][:].rearrange("p j (m t) -> p m j t", t=PACK),
+                )
+            words = keep.tile([P, H], U32, name="w1_words_%d" % z, align_bytes=64)
+            scales = keep.tile([P, H], U8, name="w1_bytes_%d" % z, align_bytes=64)
+            nc.vector.quantize_mx(out=words[:].bitcast(FP8X4), scales=scales[:], in_=woven[:])
+            return words, scales
+
+        def gather(z, first, count):
+            if z == 1 and first >= 2 * V:
+                at = (first // V - 2) * 2048
+                words = relay.tile([P, count], U32, name="late_words_%d" % first, align_bytes=64, offset=at)
+                scales = relay.tile([P, count], U8, name="late_bytes_%d" % first, align_bytes=64, offset=at + 1024)
+            else:
+                words = keep.tile([P, count], U32, name="picked_words_%d_%d" % (z, first), align_bytes=64)
+                scales = keep.tile([P, count], U8, name="picked_bytes_%d_%d" % (z, first), align_bytes=64)
+            entries = offsets[:, first // 16 : (first + count) // 16]
+            nc.vector.tensor_copy(words[:], x_words[z][:].indirect(entries))
+            nc.vector.tensor_copy(scales[:], x_bytes[z][:].indirect(entries))
+            return words, scales
+
+        banks = [
+            [psum.tile([P, PACK, VH], F32, name="bank_%d_%d" % (d, a)) for a in range(HALVES)] for d in range(D)
+        ]
+
+        def first_product(z, w, picked, first, d, a):
+            cols = slice(first + a * VH, first + (a + 1) * VH)
+            for t in range(PACK):
+                nc.tensor.matmul_mx(
+                    out=banks[d][a][:, t, :],
+                    lhsT=w[0][:, t * P : (t + 1) * P].bitcast(FP8X4),
+                    lhsT_scale=w[1][:, t * P : (t + 1) * P],
+                    rhs=picked[0][:, cols].bitcast(FP8X4),
+                    rhs_scale=picked[1][:, cols],
+                    start=(z == 0 and t == 0),
+                    stop=(z == PASSES - 1 and t == PACK - 1),
+                )
+
+        quantize_x(0)
+        w1_q0 = quantize_w1(0)
+        picked0 = gather(0, 0, S)
+        for d in range(D):
+            for a in range(HALVES):
+                first_product(0, w1_q0, picked0, d * V, d, a)
+        quantize_x(1)
+
+        h = [keep.tile([P, V * PACK], F32, name="h_%d" % d) for d in range(D)]
+        W = VH * PACK
+        picked1 = [gather(1, 0, V), gather(1, V, V)]
+        w1_q1 = quantize_w1(1)
+        picked1.extend(gather(1, d * V, V) for d in range(2, D))
+        for d, a in ((0, 0), (1, 0), (0, 1), (1, 1), (2, 0), (2, 1), (3, 0), (3, 1)):
+            first_product(1, w1_q1, picked1[d], 0, d, a)
+            nc.scalar.activation(
+                out=h[d][:, a * W : (a + 1) * W].rearrange("p (n t) -> p n t", t=PACK),
+                in_=banks[d][a][:].rearrange("p t n -> p n t"),
+                func=ACT.Gelu_apprx_tanh,
+            )
+
+        root_warm = keep.tile([P, 1], F32, name="root_warm")
+        nc.scalar.activation(out=root_warm[:], in_=h[D - 1][:, V * PACK - 1 : V * PACK], func=ACT.Sqrt, scale=0.0)
+
+        w23_q = []
+        for n in range(2):
+            woven = keep.tile([P, N * PACK], BF16, name="w23_woven_%d" % n, align_bytes=64)
+            nc.gpsimd.tensor_scalar(
+                out=woven[:].rearrange("p (c i j) -> p c j i", i=4, j=PACK),
+                in0=w23_raw[n][:].rearrange("p j (c i) -> p c j i", i=4),
+                scalar1=1.0,
+                scalar2=0.0,
+                op0=ALU.mult,
+                op1=ALU.add,
+            )
+            words = keep.tile([P, N], U32, name="w23_words_%d" % n, align_bytes=64)
+            scales = keep.tile([P, N], U8, name="w23_bytes_%d" % n, align_bytes=64)
+            nc.vector.quantize_mx(out=words[:].bitcast(FP8X4), scales=scales[:], in_=woven[:])
+            w23_q.append((words, scales))
+
+        def stat(name):
+            return keep.tile([P, V * PACK], F32, name=name)
+
+        d01, m01, d23, m23, dm = stat("d01"), stat("m01"), stat("d23"), stat("m23"), stat("dm")
+        q01, q23, qm, q_pairs, q_all = stat("q01"), stat("q23"), stat("qm"), stat("q_pairs"), stat("q_all")
+
+        def half_way(out_ap, diff, left):
+            nc.vector.scalar_tensor_tensor(out=out_ap, in0=diff, scalar=-0.5, in1=left, op0=ALU.mult, op1=ALU.add)
+
+        halves = [slice(a * W, (a + 1) * W) for a in range(HALVES)]
+        for diff, middle, square, left, right in ((d01, m01, q01, h[0], h[1]), (d23, m23, q23, h[2], h[3])):
+            for c in halves:
+                nc.vector.tensor_tensor(diff[:, c], left[:, c], right[:, c], ALU.subtract)
+                nc.scalar.activation(out=square[:, c], in_=diff[:, c], func=ACT.Square)
+            for c in halves:
+                half_way(middle[:, c], diff[:, c], left[:, c])
+        for c in halves:
+            nc.vector.tensor_tensor(dm[:, c], m01[:, c], m23[:, c], ALU.subtract)
+            nc.scalar.activation(out=qm[:, c], in_=dm[:, c], func=ACT.Square)
+        for c in halves:
+            nc.vector.tensor_tensor(q_pairs[:, c], q01[:, c], q23[:, c], ALU.add)
+        pooled = [
+            [keep.tile([P, W], BF16, name="pooled_%d_%d" % (a, n), align_bytes=64) for n in range(2)]
+            for a in range(HALVES)
+        ]
+        for a, c in enumerate(halves):
+            nc.vector.scalar_tensor_tensor(
+                out=q_all[:, c], in0=qm[:, c], scalar=2.0, in1=q_pairs[:, c], op0=ALU.mult, op1=ALU.add
+            )
+            nc.scalar.activation(out=pooled[a][1][:], in_=q_all[:, c], func=ACT.Sqrt, scale=0.125)
+
+        for a, c in enumerate(halves):
+            half_way(pooled[a][0][:], dm[:, c], m01[:, c])
+            result = keep.tile([P, N // P, VH], F32, name="result_%d" % a)
+            codes = {}
+            for n in (1, 0):
+                words = keep.tile([P, VH], U32, name="pooled_words_%d_%d" % (n, a), align_bytes=64)
+                scales = keep.tile([P, VH], U8, name="pooled_bytes_%d_%d" % (n, a), align_bytes=64)
+                nc.vector.quantize_mx(out=words[:].bitcast(FP8X4), scales=scales[:], in_=pooled[a][n][:])
+                codes[n] = (words, scales)
+            for b in range(N // P):
+                acc = psum.tile([P, VH], F32, name="bank_%d_%d" % (b, a))
+                for n in (1, 0):
+                    nc.tensor.matmul_mx(
+                        out=acc[:],
+                        lhsT=w23_q[n][0][:, b * P : (b + 1) * P].bitcast(FP8X4),
+                        lhsT_scale=w23_q[n][1][:, b * P : (b + 1) * P],
+                        rhs=codes[n][0][:].bitcast(FP8X4),
+                        rhs_scale=codes[n][1][:],
+                        start=(n == 1),
+                        stop=(n == 0),
+                    )
+                weave(nc, b == 0, result[:, b, :], acc[:])
+            nc.sync.dma_start(
+                out=out[:, a * VH : (a + 1) * VH].rearrange("(b p) v -> p b v", p=P), in_=result[:]
+            )

@@ -1,6 +1,7 @@
 from contextlib import ExitStack
 
 import concourse.mybir as mybir
+from concourse.masks import make_identity
 
 K, T, S, V, H, N = 1024, 2048, 1024, 256, 512, 256
 D = S // V
@@ -20,13 +21,14 @@ P = 128
 PACK = 4
 K_PASS = P * PACK
 PASSES = K // K_PASS
-VH = 128
-HALVES = V // VH
-CHUNKS = ((512, 512, 512, 512), (512, 512, 512, 256, 256))
-VECTOR_COLUMNS = ((0, 512, 0, 512), (0, 0, 256, 128, 160))
+HALVES = V // P
+HH = H // 2
+CHUNKS = ((512, 512, 512, 512), (512, 512, 512, 256, 128, 128))
+VECTOR_COLUMNS = ((320, 320, 320, 320), (0, 256, 256, 128, 0, 64))
+SCALE_ROW = (0, 4)
 
 
-def weave(nc, on_vector, out, in_):
+def copy_on(nc, on_vector, out, in_):
     if on_vector:
         nc.vector.tensor_copy(out=out, in_=in_)
     else:
@@ -43,8 +45,11 @@ def tile_picked_statpool_gelu_e_kernel(tc, xT, w1, w2, w3, offs, out):
 
         offsets = keep.tile([P, S // 16], U16, name="offsets")
 
-        def load(rows, name):
-            raw = keep.tile([P, PACK, rows.shape[1]], F32, name=name)
+        def load(rows, name, at=None):
+            if at is None:
+                raw = keep.tile([P, PACK, rows.shape[1]], F32, name=name)
+            else:
+                raw = relay.tile([P, PACK, rows.shape[1]], F32, name=name, align_bytes=64, offset=at)
             nc.sync.dma_start(out=raw[:], in_=rows.rearrange("(p j) w -> p j w", j=PACK))
             return raw
 
@@ -57,19 +62,28 @@ def tile_picked_statpool_gelu_e_kernel(tc, xT, w1, w2, w3, offs, out):
 
         x_raw = [load_x(0)]
         nc.sync.dma_start(offsets[:], offs)
-        w1_raw = [[load(w1[0:K_PASS, :], "w1_raw_0")]]
         x_raw.append(load_x(1))
-        w1_raw.append([load(w1[K_PASS:K, u * 256 : (u + 1) * 256], "w1_raw_1_%d" % u) for u in range(2)])
-        w23_raw = [load(w2, "w2_raw"), load(w3, "w3_raw")]
+        raw_at = {(0, 0): None, (0, 1): None, (1, 0): None, (1, 1): 8192}
+        w1_raw = [
+            [
+                load(w1[z * K_PASS : (z + 1) * K_PASS, u * HH : (u + 1) * HH], "w1_raw_%d_%d" % (u, z), raw_at[u, z])
+                for z in range(PASSES)
+            ]
+            for u in range(2)
+        ]
+        w23_raw = keep.tile([P, PACK, 2, N], F32, name="w23_raw")
+        for n, w in enumerate((w2, w3)):
+            nc.sync.dma_start(out=w23_raw[:, :, n, :], in_=w.rearrange("(p j) w -> p j w", j=PACK))
 
         warm = keep.tile([P, 2], F32, name="warm")
         nc.gpsimd.memset(warm[:, 0:1], 0.0)
         nc.scalar.activation(out=warm[:, 1:2], in_=warm[:, 0:1], func=ACT.Gelu_apprx_tanh)
+        identity = keep.tile([P, P], F32, name="identity")
+        make_identity(nc, identity[:])
 
         x_words = [keep.tile([P, T], U32, name="x_words_%d" % z, align_bytes=64) for z in range(PASSES)]
-        x_bytes = [keep.tile([P, T], U8, name="x_bytes_%d" % z, align_bytes=64) for z in range(PASSES)]
-        for z in range(PASSES):
-            nc.gpsimd.memset(x_bytes[z][:].bitcast(I32), 0)
+        x_bytes = keep.tile([P, T], U8, name="x_bytes", align_bytes=64)
+        nc.gpsimd.memset(x_bytes[:].bitcast(I32), 0)
 
         def quantize_x(z):
             c0 = 0
@@ -78,7 +92,7 @@ def tile_picked_statpool_gelu_e_kernel(tc, xT, w1, w2, w3, offs, out):
                 cut = VECTOR_COLUMNS[z][n]
                 for on_vector, lo, hi in ((True, 0, cut), (False, cut, width)):
                     if hi > lo:
-                        weave(
+                        copy_on(
                             nc,
                             on_vector,
                             woven[:, lo * PACK : hi * PACK].rearrange("p (c i j) -> p c j i", i=4, j=PACK),
@@ -86,152 +100,206 @@ def tile_picked_statpool_gelu_e_kernel(tc, xT, w1, w2, w3, offs, out):
                         )
                 nc.vector.quantize_mx(
                     out=x_words[z][:, c0 : c0 + width].bitcast(FP8X4),
-                    scales=x_bytes[z][:, c0 : c0 + width],
+                    scales=x_bytes[SCALE_ROW[z] : P, c0 : c0 + width],
                     in_=woven[:],
                 )
                 c0 += width
 
-        def quantize_w1(z):
-            if z == 0:
-                woven = keep.tile([P, H * PACK], BF16, name="w1_woven_0", align_bytes=64)
-            else:
-                woven = relay.tile([P, H * PACK], BF16, name="w1_woven_1", align_bytes=64, offset=0)
-            view = woven[:].rearrange("p (t m j) -> p m j t", t=PACK, j=PACK)
-            parts = len(w1_raw[z])
-            for u in range(parts):
-                m = P // parts
-                nc.scalar.copy(
-                    out=view[:, u * m : (u + 1) * m],
-                    in_=w1_raw[z][u][:].rearrange("p j (m t) -> p m j t", t=PACK),
-                )
-            words = keep.tile([P, H], U32, name="w1_words_%d" % z, align_bytes=64)
-            scales = keep.tile([P, H], U8, name="w1_bytes_%d" % z, align_bytes=64)
-            nc.vector.quantize_mx(out=words[:].bitcast(FP8X4), scales=scales[:], in_=woven[:])
+        def quantized(name, woven, width):
+            words = keep.tile([P, width], U32, name=name + "_words", align_bytes=64)
+            scales = keep.tile([P, width], U8, name=name + "_bytes", align_bytes=64)
+            nc.vector.quantize_mx(out=words[:].bitcast(FP8X4), scales=scales[:], in_=woven)
             return words, scales
 
-        def gather(z, first, count):
-            if z == 1 and first >= 2 * V:
-                at = (first // V - 2) * 2048
-                words = relay.tile([P, count], U32, name="late_words_%d" % first, align_bytes=64, offset=at)
-                scales = relay.tile([P, count], U8, name="late_bytes_%d" % first, align_bytes=64, offset=at + 1024)
-            else:
-                words = keep.tile([P, count], U32, name="picked_words_%d_%d" % (z, first), align_bytes=64)
-                scales = keep.tile([P, count], U8, name="picked_bytes_%d_%d" % (z, first), align_bytes=64)
-            entries = offsets[:, first // 16 : (first + count) // 16]
-            nc.vector.tensor_copy(words[:], x_words[z][:].indirect(entries))
-            nc.vector.tensor_copy(scales[:], x_bytes[z][:].indirect(entries))
-            return words, scales
+        def weave_w1(woven, raw):
+            nc.scalar.copy(
+                out=woven.rearrange("p (t m j) -> p m j t", t=PACK, j=PACK),
+                in_=raw.rearrange("p j (m t) -> p m j t", t=PACK),
+            )
 
-        banks = [
-            [psum.tile([P, PACK, VH], F32, name="bank_%d_%d" % (d, a)) for a in range(HALVES)] for d in range(D)
-        ]
+        def picked_tile(name, dtype, count, at):
+            if at is None:
+                return keep.tile([P, count], dtype, name=name, align_bytes=64)
+            return relay.tile([P, count], dtype, name=name, align_bytes=64, offset=at)
 
-        def first_product(z, w, picked, first, d, a):
-            cols = slice(first + a * VH, first + (a + 1) * VH)
-            for t in range(PACK):
-                nc.tensor.matmul_mx(
-                    out=banks[d][a][:, t, :],
-                    lhsT=w[0][:, t * P : (t + 1) * P].bitcast(FP8X4),
-                    lhsT_scale=w[1][:, t * P : (t + 1) * P],
-                    rhs=picked[0][:, cols].bitcast(FP8X4),
-                    rhs_scale=picked[1][:, cols],
-                    start=(z == 0 and t == 0),
-                    stop=(z == PASSES - 1 and t == PACK - 1),
-                )
+        def gather(window, name, dtype, first, count, at=None):
+            picked = picked_tile(name, dtype, count, at)
+            nc.vector.tensor_copy(picked[:], window[:].indirect(offsets[:, first // 16 : (first + count) // 16]))
+            return picked
+
+        banks = [[psum.tile([P, HALVES, HH], F32, name="bank_%d_%d" % (d, u)) for u in range(2)] for d in range(D)]
 
         quantize_x(0)
-        w1_q0 = quantize_w1(0)
-        picked0 = gather(0, 0, S)
-        for d in range(D):
-            for a in range(HALVES):
-                first_product(0, w1_q0, picked0, d * V, d, a)
+        words0 = gather(x_words[0], "picked_words_0", U32, 0, S)
         quantize_x(1)
 
-        h = [keep.tile([P, V * PACK], F32, name="h_%d" % d) for d in range(D)]
-        W = VH * PACK
-        picked1 = [gather(1, 0, V), gather(1, V, V)]
-        w1_q1 = quantize_w1(1)
-        picked1.extend(gather(1, d * V, V) for d in range(2, D))
-        for d, a in ((0, 0), (1, 0), (0, 1), (1, 1), (2, 0), (2, 1), (3, 0), (3, 1)):
-            first_product(1, w1_q1, picked1[d], 0, d, a)
+        words_at = (0, 1024, 20480, 21760)
+        bytes_at = (None, 2048, 21504)
+        woven_at = {(0, 0): 0, (0, 1): None, (1, 0): 2048, (1, 1): 20480}
+        w1_woven = {}
+        for u in range(2):
+            for z in range(PASSES):
+                w1_woven[u, z] = picked_tile("w1_woven_%d_%d" % (u, z), BF16, HH * PACK, woven_at[u, z])
+                weave_w1(w1_woven[u, z][:], w1_raw[u][z][:])
+        words1, scales, w1_q = [], {}, {}
+
+        def gather_words(d):
+            words1.append(gather(x_words[1], "picked_words_1_%d" % d, U32, d * V, V, words_at[d]))
+
+        def gather_bytes(first, pieces, at):
+            picked = gather(x_bytes, "picked_bytes_%d" % first, U8, first * V, pieces * V, at)
+            for d in range(pieces):
+                scales[first + d] = (picked, d * V)
+
+        def quantize_w1(u, z):
+            w1_q[u, z] = quantized("w1_%d_%d" % (u, z), w1_woven[u, z][:], HH)
+
+        gather_bytes(0, 2, bytes_at[0])
+        quantize_w1(0, 0)
+        gather_words(0)
+        gather_words(1)
+        quantize_w1(0, 1)
+        quantize_w1(1, 0)
+        gather_bytes(2, 1, bytes_at[1])
+        quantize_w1(1, 1)
+        gather_words(2)
+        gather_bytes(3, 1, bytes_at[2])
+        gather_words(3)
+
+        def first_product(z, d, u):
+            for a in range(HALVES):
+                cols = slice(a * P, (a + 1) * P)
+                words = words0[:, d * V + a * P : d * V + (a + 1) * P] if z == 0 else words1[d][:, cols]
+                nc.tensor.matmul_mx(
+                    out=banks[d][u][:, a, :],
+                    lhsT=words.bitcast(FP8X4),
+                    lhsT_scale=scales[d][0][SCALE_ROW[z] : P, scales[d][1] + a * P : scales[d][1] + (a + 1) * P],
+                    rhs=w1_q[u, z][0][:].bitcast(FP8X4),
+                    rhs_scale=w1_q[u, z][1][:],
+                    start=(z == 0 and a == 0),
+                    stop=(z == PASSES - 1 and a == HALVES - 1),
+                )
+
+        h = [picked_tile("h_%d" % d, F32, HALVES * H, (6144, 10240, None, 16384)[d]) for d in range(D)]
+
+        def gelu(d, u):
             nc.scalar.activation(
-                out=h[d][:, a * W : (a + 1) * W].rearrange("p (n t) -> p n t", t=PACK),
-                in_=banks[d][a][:].rearrange("p t n -> p n t"),
+                out=h[d][:].rearrange("p (g u m) -> p g u m", u=2, m=HH // PACK)[:, :, u, :],
+                in_=banks[d][u][:].rearrange("p a (t m) -> p (a t) m", t=PACK),
                 func=ACT.Gelu_apprx_tanh,
             )
 
-        root_warm = keep.tile([P, 1], F32, name="root_warm")
-        nc.scalar.activation(out=root_warm[:], in_=h[D - 1][:, V * PACK - 1 : V * PACK], func=ACT.Sqrt, scale=0.0)
+        for d in range(2):
+            first_product(0, d, 0)
+        for d in range(2):
+            first_product(1, d, 0)
+            gelu(d, 0)
+        for d, u in ((0, 1), (1, 1), (2, 0), (3, 0), (2, 1), (3, 1)):
+            first_product(0, d, u)
+            first_product(1, d, u)
+            gelu(d, u)
 
-        w23_q = []
-        for n in range(2):
-            woven = keep.tile([P, N * PACK], BF16, name="w23_woven_%d" % n, align_bytes=64)
-            nc.gpsimd.tensor_scalar(
-                out=woven[:].rearrange("p (c i j) -> p c j i", i=4, j=PACK),
-                in0=w23_raw[n][:].rearrange("p j (c i) -> p c j i", i=4),
-                scalar1=1.0,
-                scalar2=0.0,
-                op0=ALU.mult,
-                op1=ALU.add,
-            )
-            words = keep.tile([P, N], U32, name="w23_words_%d" % n, align_bytes=64)
-            scales = keep.tile([P, N], U8, name="w23_bytes_%d" % n, align_bytes=64)
-            nc.vector.quantize_mx(out=words[:].bitcast(FP8X4), scales=scales[:], in_=woven[:])
-            w23_q.append((words, scales))
+        root_warm = keep.tile([P, 1], F32, name="root_warm")
+        nc.scalar.activation(out=root_warm[:], in_=h[D - 1][:, HALVES * H - 1 : HALVES * H], func=ACT.Sqrt, scale=0.0)
 
         def stat(name):
-            return keep.tile([P, V * PACK], F32, name=name)
+            return keep.tile([P, HALVES * H], F32, name=name)
 
-        d01, m01, d23, m23, dm = stat("d01"), stat("m01"), stat("d23"), stat("m23"), stat("dm")
-        q01, q23, qm, q_pairs, q_all = stat("q01"), stat("q23"), stat("qm"), stat("q_pairs"), stat("q_all")
+        d01, s01, d23, s23, dm = stat("d01"), stat("s01"), stat("d23"), stat("s23"), stat("dm")
+        q01, q23, qm = stat("q01"), stat("q23"), stat("qm")
+        halves = [slice(a * H, (a + 1) * H) for a in range(HALVES)]
+        sum_t = [psum.tile([P, PACK, P], F32, name="bank_%d_0" % a) for a in range(HALVES)]
+        var_t = [psum.tile([P, PACK, P], F32, name="bank_%d_1" % a) for a in range(HALVES)]
 
-        def half_way(out_ap, diff, left):
-            nc.vector.scalar_tensor_tensor(out=out_ap, in0=diff, scalar=-0.5, in1=left, op0=ALU.mult, op1=ALU.add)
+        def turn(bank, source, a, first, last):
+            for t in range(PACK):
+                nc.tensor.matmul(
+                    bank[:, t, :],
+                    source[:, a * H + t * P : a * H + (t + 1) * P],
+                    identity[:],
+                    is_transpose=True,
+                    start=(first and t == 0),
+                    stop=(last and t == PACK - 1),
+                )
 
-        halves = [slice(a * W, (a + 1) * W) for a in range(HALVES)]
-        for diff, middle, square, left, right in ((d01, m01, q01, h[0], h[1]), (d23, m23, q23, h[2], h[3])):
-            for c in halves:
-                nc.vector.tensor_tensor(diff[:, c], left[:, c], right[:, c], ALU.subtract)
-                nc.scalar.activation(out=square[:, c], in_=diff[:, c], func=ACT.Square)
-            for c in halves:
-                half_way(middle[:, c], diff[:, c], left[:, c])
-        for c in halves:
-            nc.vector.tensor_tensor(dm[:, c], m01[:, c], m23[:, c], ALU.subtract)
-            nc.scalar.activation(out=qm[:, c], in_=dm[:, c], func=ACT.Square)
-        for c in halves:
-            nc.vector.tensor_tensor(q_pairs[:, c], q01[:, c], q23[:, c], ALU.add)
+        def hidden_half(tile, u):
+            return tile[:].rearrange("p (g u m) -> p g u m", u=2, m=HH // PACK)[:, :, u, :]
+
+        def combine(result, left, right, u, op):
+            nc.vector.tensor_tensor(hidden_half(result, u), hidden_half(left, u), hidden_half(right, u), op)
+
+        for u in range(2):
+            combine(s01, h[0], h[1], u, ALU.add)
+            combine(d01, h[0], h[1], u, ALU.subtract)
+        for u in range(2):
+            combine(s23, h[2], h[3], u, ALU.add)
+            combine(d23, h[2], h[3], u, ALU.subtract)
+            combine(dm, s01, s23, u, ALU.subtract)
+        for a in range(HALVES):
+            turn(sum_t[a], s01, a, True, False)
+        for a in range(HALVES):
+            turn(sum_t[a], s23, a, False, True)
+        nc.scalar.activation(out=q01[:], in_=d01[:], func=ACT.Square)
+        for a in range(HALVES):
+            turn(var_t[a], q01, a, True, False)
+        for a, c in enumerate(halves):
+            nc.scalar.activation(out=q23[:, c], in_=d23[:, c], func=ACT.Square)
+            turn(var_t[a], q23, a, False, False)
+            nc.scalar.activation(out=qm[:, c], in_=dm[:, c], func=ACT.Square, scale=0.5**0.5)
+            turn(var_t[a], qm, a, False, True)
+
         pooled = [
-            [keep.tile([P, W], BF16, name="pooled_%d_%d" % (a, n), align_bytes=64) for n in range(2)]
+            [keep.tile([P, H], BF16, name="pooled_%d_%d" % (a, n), align_bytes=64) for n in range(2)]
             for a in range(HALVES)
         ]
-        for a, c in enumerate(halves):
-            nc.vector.scalar_tensor_tensor(
-                out=q_all[:, c], in0=qm[:, c], scalar=2.0, in1=q_pairs[:, c], op0=ALU.mult, op1=ALU.add
-            )
-            nc.scalar.activation(out=pooled[a][1][:], in_=q_all[:, c], func=ACT.Sqrt, scale=0.125)
 
-        for a, c in enumerate(halves):
-            half_way(pooled[a][0][:], dm[:, c], m01[:, c])
-            result = keep.tile([P, N // P, VH], F32, name="result_%d" % a)
-            codes = {}
-            for n in (1, 0):
-                words = keep.tile([P, VH], U32, name="pooled_words_%d_%d" % (n, a), align_bytes=64)
-                scales = keep.tile([P, VH], U8, name="pooled_bytes_%d_%d" % (n, a), align_bytes=64)
-                nc.vector.quantize_mx(out=words[:].bitcast(FP8X4), scales=scales[:], in_=pooled[a][n][:])
-                codes[n] = (words, scales)
-            for b in range(N // P):
-                acc = psum.tile([P, VH], F32, name="bank_%d_%d" % (b, a))
-                for n in (1, 0):
-                    nc.tensor.matmul_mx(
-                        out=acc[:],
-                        lhsT=w23_q[n][0][:, b * P : (b + 1) * P].bitcast(FP8X4),
-                        lhsT_scale=w23_q[n][1][:, b * P : (b + 1) * P],
-                        rhs=codes[n][0][:].bitcast(FP8X4),
-                        rhs_scale=codes[n][1][:],
-                        start=(n == 1),
-                        stop=(n == 0),
-                    )
-                weave(nc, b == 0, result[:, b, :], acc[:])
-            nc.sync.dma_start(
-                out=out[:, a * VH : (a + 1) * VH].rearrange("(b p) v -> p b v", p=P), in_=result[:]
+        def mean(a):
+            nc.vector.tensor_scalar(
+                out=pooled[a][0][:].rearrange("p (v t) -> p v t", t=PACK),
+                in0=sum_t[a][:].rearrange("p t v -> p v t"),
+                scalar1=0.25,
+                scalar2=None,
+                op0=ALU.mult,
             )
+
+        w23_woven = relay.tile([P, 2 * N * PACK], BF16, name="w23_woven", align_bytes=64, offset=16384)
+        nc.vector.tensor_copy(
+            out=w23_woven[:].rearrange("p (c i j) -> p c j i", i=4, j=PACK),
+            in_=w23_raw[:].rearrange("p j n (c i) -> p (n c) j i", i=4),
+        )
+        mean(0)
+        w23_q = quantized("w23", w23_woven[:], 2 * N)
+        mean(1)
+        for a in range(HALVES):
+            nc.scalar.activation(
+                out=pooled[a][1][:].rearrange("p (v t) -> p v t", t=PACK),
+                in_=var_t[a][:].rearrange("p t v -> p v t"),
+                func=ACT.Sqrt,
+                scale=0.125,
+            )
+        sums = [
+            [psum.tile([P, P], F32, name="bank_%d_%d" % (2 + a, b)) for b in range(N // P)] for a in range(HALVES)
+        ]
+
+        def second_product(n, a):
+            words, scales = quantized("pooled_%d_%d" % (a, n), pooled[a][n][:], P)
+            for b in range(N // P):
+                cols = slice(n * N + b * P, n * N + (b + 1) * P)
+                nc.tensor.matmul_mx(
+                    out=sums[a][b][:],
+                    lhsT=w23_q[0][:, cols].bitcast(FP8X4),
+                    lhsT_scale=w23_q[1][:, cols],
+                    rhs=words[:].bitcast(FP8X4),
+                    rhs_scale=scales[:],
+                    start=(n == 0),
+                    stop=(n == 1),
+                )
+
+        for n in range(2):
+            for a in range(HALVES):
+                second_product(n, a)
+        for a in range(HALVES):
+            result = keep.tile([P, N // P, P], F32, name="result_%d" % a)
+            for b in range(N // P):
+                copy_on(nc, b == 0, result[:, b, :], sums[a][b][:])
+            nc.sync.dma_start(out=out[:, a * P : (a + 1) * P].rearrange("(b p) v -> p b v", p=P), in_=result[:])

from contextlib import ExitStack

import concourse.mybir as mybir
from concourse.masks import make_identity

K, T, S, V, H, N = 1024, 2048, 1024, 256, 512, 256
D = S // V
FLOPS = 2 * K * H * S + 2 * 2 * H * N * V

F32 = mybir.dt.float32
BF16 = mybir.dt.bfloat16
I32 = mybir.dt.int32
U32 = mybir.dt.uint32
U16 = mybir.dt.uint16
U8 = mybir.dt.uint8
FP8X4 = mybir.dt.float8_e4m3fn_x4
ACT = mybir.ActivationFunctionType
ALU = mybir.AluOpType

P = 128
PACK = 4
K_PASS = P * PACK
PASSES = K // K_PASS
HALVES = V // P
HH = H // 2
CHUNKS = ((512, 512, 512, 512), (512, 512, 512, 256, 128, 128))
VECTOR_COLUMNS = ((320, 320, 320, 320), (0, 256, 256, 128, 0, 64))
SCALE_ROW = (0, 4)


def copy_on(nc, on_vector, out, in_):
    if on_vector:
        nc.vector.tensor_copy(out=out, in_=in_)
    else:
        nc.scalar.copy(out=out, in_=in_)


def tile_picked_statpool_gelu_e_kernel(tc, xT, w1, w2, w3, offs, out):
    nc = tc.nc
    with ExitStack() as ctx:
        keep = ctx.enter_context(tc.tile_pool(name="keep", bufs=1))
        ring = ctx.enter_context(tc.tile_pool(name="ring", bufs=3))
        relay = ctx.enter_context(tc.tile_pool(name="relay", bufs=1))
        psum = ctx.enter_context(tc.psum_pool(name="psum", bufs=1))

        offsets = keep.tile([P, S // 16], U16, name="offsets")

        def load(rows, name, at=None):
            if at is None:
                raw = keep.tile([P, PACK, rows.shape[1]], F32, name=name)
            else:
                raw = relay.tile([P, PACK, rows.shape[1]], F32, name=name, align_bytes=64, offset=at)
            nc.sync.dma_start(out=raw[:], in_=rows.rearrange("(p j) w -> p j w", j=PACK))
            return raw

        def load_x(z):
            tiles, c0 = [], 0
            for n, width in enumerate(CHUNKS[z]):
                tiles.append(load(xT[z * K_PASS : (z + 1) * K_PASS, c0 : c0 + width], "x_raw_%d_%d" % (z, n)))
                c0 += width
            return tiles

        x_raw = [load_x(0)]
        nc.sync.dma_start(offsets[:], offs)
        x_raw.append(load_x(1))
        raw_at = {(0, 0): None, (0, 1): None, (1, 0): None, (1, 1): 8192}
        w1_raw = [
            [
                load(w1[z * K_PASS : (z + 1) * K_PASS, u * HH : (u + 1) * HH], "w1_raw_%d_%d" % (u, z), raw_at[u, z])
                for z in range(PASSES)
            ]
            for u in range(2)
        ]
        w23_raw = keep.tile([P, PACK, 2, N], F32, name="w23_raw")
        for n, w in enumerate((w2, w3)):
            nc.sync.dma_start(out=w23_raw[:, :, n, :], in_=w.rearrange("(p j) w -> p j w", j=PACK))

        warm = keep.tile([P, 2], F32, name="warm")
        nc.gpsimd.memset(warm[:, 0:1], 0.0)
        nc.scalar.activation(out=warm[:, 1:2], in_=warm[:, 0:1], func=ACT.Gelu_apprx_tanh)
        identity = keep.tile([P, P], F32, name="identity")
        make_identity(nc, identity[:])

        x_words = [keep.tile([P, T], U32, name="x_words_%d" % z, align_bytes=64) for z in range(PASSES)]
        x_bytes = keep.tile([P, T], U8, name="x_bytes", align_bytes=64)
        nc.gpsimd.memset(x_bytes[:].bitcast(I32), 0)

        def quantize_x(z):
            c0 = 0
            for n, width in enumerate(CHUNKS[z]):
                woven = ring.tile([P, width * PACK], BF16, name="x_woven", align_bytes=64)
                cut = VECTOR_COLUMNS[z][n]
                for on_vector, lo, hi in ((True, 0, cut), (False, cut, width)):
                    if hi > lo:
                        copy_on(
                            nc,
                            on_vector,
                            woven[:, lo * PACK : hi * PACK].rearrange("p (c i j) -> p c j i", i=4, j=PACK),
                            x_raw[z][n][:, :, lo:hi].rearrange("p j (c i) -> p c j i", i=4),
                        )
                nc.vector.quantize_mx(
                    out=x_words[z][:, c0 : c0 + width].bitcast(FP8X4),
                    scales=x_bytes[SCALE_ROW[z] : P, c0 : c0 + width],
                    in_=woven[:],
                )
                c0 += width

        def quantized(name, woven, width):
            words = keep.tile([P, width], U32, name=name + "_words", align_bytes=64)
            scales = keep.tile([P, width], U8, name=name + "_bytes", align_bytes=64)
            nc.vector.quantize_mx(out=words[:].bitcast(FP8X4), scales=scales[:], in_=woven)
            return words, scales

        def weave_w1(woven, raw):
            nc.scalar.copy(
                out=woven.rearrange("p (t m j) -> p m j t", t=PACK, j=PACK),
                in_=raw.rearrange("p j (m t) -> p m j t", t=PACK),
            )

        def picked_tile(name, dtype, count, at):
            if at is None:
                return keep.tile([P, count], dtype, name=name, align_bytes=64)
            return relay.tile([P, count], dtype, name=name, align_bytes=64, offset=at)

        def gather(window, name, dtype, first, count, at=None):
            picked = picked_tile(name, dtype, count, at)
            nc.vector.tensor_copy(picked[:], window[:].indirect(offsets[:, first // 16 : (first + count) // 16]))
            return picked

        banks = [[psum.tile([P, HALVES, HH], F32, name="bank_%d_%d" % (d, u)) for u in range(2)] for d in range(D)]

        quantize_x(0)
        words0 = gather(x_words[0], "picked_words_0", U32, 0, S)
        quantize_x(1)

        words_at = (0, 1024, 20480, 21760)
        bytes_at = (None, 2048, 21504)
        woven_at = {(0, 0): 0, (0, 1): None, (1, 0): 2048, (1, 1): 20480}
        w1_woven = {}
        for u in range(2):
            for z in range(PASSES):
                w1_woven[u, z] = picked_tile("w1_woven_%d_%d" % (u, z), BF16, HH * PACK, woven_at[u, z])
                weave_w1(w1_woven[u, z][:], w1_raw[u][z][:])
        words1, scales, w1_q = [], {}, {}

        def gather_words(d):
            words1.append(gather(x_words[1], "picked_words_1_%d" % d, U32, d * V, V, words_at[d]))

        def gather_bytes(first, pieces, at):
            picked = gather(x_bytes, "picked_bytes_%d" % first, U8, first * V, pieces * V, at)
            for d in range(pieces):
                scales[first + d] = (picked, d * V)

        def quantize_w1(u, z):
            w1_q[u, z] = quantized("w1_%d_%d" % (u, z), w1_woven[u, z][:], HH)

        gather_bytes(0, 2, bytes_at[0])
        quantize_w1(0, 0)
        gather_words(0)
        gather_words(1)
        quantize_w1(0, 1)
        quantize_w1(1, 0)
        gather_bytes(2, 1, bytes_at[1])
        quantize_w1(1, 1)
        gather_words(2)
        gather_bytes(3, 1, bytes_at[2])
        gather_words(3)

        def first_product(z, d, u):
            for a in range(HALVES):
                cols = slice(a * P, (a + 1) * P)
                words = words0[:, d * V + a * P : d * V + (a + 1) * P] if z == 0 else words1[d][:, cols]
                nc.tensor.matmul_mx(
                    out=banks[d][u][:, a, :],
                    lhsT=words.bitcast(FP8X4),
                    lhsT_scale=scales[d][0][SCALE_ROW[z] : P, scales[d][1] + a * P : scales[d][1] + (a + 1) * P],
                    rhs=w1_q[u, z][0][:].bitcast(FP8X4),
                    rhs_scale=w1_q[u, z][1][:],
                    start=(z == 0 and a == 0),
                    stop=(z == PASSES - 1 and a == HALVES - 1),
                )

        h = [picked_tile("h_%d" % d, F32, HALVES * H, (6144, 10240, None, 16384)[d]) for d in range(D)]

        def gelu(d, u):
            nc.scalar.activation(
                out=h[d][:].rearrange("p (g u m) -> p g u m", u=2, m=HH // PACK)[:, :, u, :],
                in_=banks[d][u][:].rearrange("p a (t m) -> p (a t) m", t=PACK),
                func=ACT.Gelu_apprx_tanh,
            )

        for d in range(2):
            first_product(0, d, 0)
        for d in range(2):
            first_product(1, d, 0)
            gelu(d, 0)
        for d, u in ((0, 1), (1, 1), (2, 0), (3, 0), (2, 1), (3, 1)):
            first_product(0, d, u)
            first_product(1, d, u)
            gelu(d, u)

        root_warm = keep.tile([P, 1], F32, name="root_warm")
        nc.scalar.activation(out=root_warm[:], in_=h[D - 1][:, HALVES * H - 1 : HALVES * H], func=ACT.Sqrt, scale=0.0)

        def stat(name):
            return keep.tile([P, HALVES * H], F32, name=name)

        d01, s01, d23, s23, dm = stat("d01"), stat("s01"), stat("d23"), stat("s23"), stat("dm")
        q01, q23, qm = stat("q01"), stat("q23"), stat("qm")
        halves = [slice(a * H, (a + 1) * H) for a in range(HALVES)]
        sum_t = [psum.tile([P, PACK, P], F32, name="bank_%d_0" % a) for a in range(HALVES)]
        var_t = [psum.tile([P, PACK, P], F32, name="bank_%d_1" % a) for a in range(HALVES)]

        def turn(bank, source, a, first, last):
            for t in range(PACK):
                nc.tensor.matmul(
                    bank[:, t, :],
                    source[:, a * H + t * P : a * H + (t + 1) * P],
                    identity[:],
                    is_transpose=True,
                    start=(first and t == 0),
                    stop=(last and t == PACK - 1),
                )

        def hidden_half(tile, u):
            return tile[:].rearrange("p (g u m) -> p g u m", u=2, m=HH // PACK)[:, :, u, :]

        def combine(result, left, right, u, op):
            nc.vector.tensor_tensor(hidden_half(result, u), hidden_half(left, u), hidden_half(right, u), op)

        for u in range(2):
            combine(s01, h[0], h[1], u, ALU.add)
            combine(d01, h[0], h[1], u, ALU.subtract)
        for u in range(2):
            combine(s23, h[2], h[3], u, ALU.add)
            combine(d23, h[2], h[3], u, ALU.subtract)
            combine(dm, s01, s23, u, ALU.subtract)
        for a in range(HALVES):
            turn(sum_t[a], s01, a, True, False)
        for a in range(HALVES):
            turn(sum_t[a], s23, a, False, True)
        nc.scalar.activation(out=q01[:], in_=d01[:], func=ACT.Square)
        for a in range(HALVES):
            turn(var_t[a], q01, a, True, False)
        for a, c in enumerate(halves):
            nc.scalar.activation(out=q23[:, c], in_=d23[:, c], func=ACT.Square)
            turn(var_t[a], q23, a, False, False)
            nc.scalar.activation(out=qm[:, c], in_=dm[:, c], func=ACT.Square, scale=0.5**0.5)
            turn(var_t[a], qm, a, False, True)

        pooled = [
            [keep.tile([P, H], BF16, name="pooled_%d_%d" % (a, n), align_bytes=64) for n in range(2)]
            for a in range(HALVES)
        ]

        def mean(a):
            nc.vector.tensor_scalar(
                out=pooled[a][0][:].rearrange("p (v t) -> p v t", t=PACK),
                in0=sum_t[a][:].rearrange("p t v -> p v t"),
                scalar1=0.25,
                scalar2=None,
                op0=ALU.mult,
            )

        w23_woven = relay.tile([P, 2 * N * PACK], BF16, name="w23_woven", align_bytes=64, offset=16384)
        nc.vector.tensor_copy(
            out=w23_woven[:].rearrange("p (c i j) -> p c j i", i=4, j=PACK),
            in_=w23_raw[:].rearrange("p j n (c i) -> p (n c) j i", i=4),
        )
        mean(0)
        w23_q = quantized("w23", w23_woven[:], 2 * N)
        mean(1)
        for a in range(HALVES):
            nc.scalar.activation(
                out=pooled[a][1][:].rearrange("p (v t) -> p v t", t=PACK),
                in_=var_t[a][:].rearrange("p t v -> p v t"),
                func=ACT.Sqrt,
                scale=0.125,
            )
        sums = [
            [psum.tile([P, P], F32, name="bank_%d_%d" % (2 + a, b)) for b in range(N // P)] for a in range(HALVES)
        ]

        def second_product(n, a):
            words, scales = quantized("pooled_%d_%d" % (a, n), pooled[a][n][:], P)
            for b in range(N // P):
                cols = slice(n * N + b * P, n * N + (b + 1) * P)
                nc.tensor.matmul_mx(
                    out=sums[a][b][:],
                    lhsT=w23_q[0][:, cols].bitcast(FP8X4),
                    lhsT_scale=w23_q[1][:, cols],
                    rhs=words[:].bitcast(FP8X4),
                    rhs_scale=scales[:],
                    start=(n == 0),
                    stop=(n == 1),
                )

        for n in range(2):
            for a in range(HALVES):
                second_product(n, a)
        for a in range(HALVES):
            result = keep.tile([P, N // P, P], F32, name="result_%d" % a)
            for b in range(N // P):
                copy_on(nc, b == 0, result[:, b, :], sums[a][b][:])
            nc.sync.dma_start(out=out[:, a * P : (a + 1) * P].rearrange("(b p) v -> p b v", p=P), in_=result[:])
